import numpy as np, ml_dtypes
CORES = [3,5,19,21,35,37,51,53,67,69]
N = 10
GR, GC = 2, 5
L, KA, KB, F = 20, 4, 10, 256
def setup_inputs(rng):
    return {"a": rng.standard_normal((N, 128, KA * 128), dtype=np.float32).astype(ml_dtypes.bfloat16), "b": rng.standard_normal((N, 128, KB * F), dtype=np.float32).astype(ml_dtypes.bfloat16)}
def reference(a, b):
    A, B = a.astype(np.float64), b.astype(np.float64)
    y = np.zeros((N, 128, F))
    for i in range(GR):
        for j in range(GC):
            for k in range(L):
                At = A[i * GC + k // KA][:, 128 * (k % KA):128 * (k % KA) + 128]
                Bt = B[(k // KB) * GC + j][:, F * (k % KB):F * (k % KB) + F]
                y[i * GC + j] += At.T @ Bt
    return {"y": y.astype(ml_dtypes.bfloat16 if a.dtype != np.float64 else np.float64)}

from concourse.mybir import AluOpType

N, GR, GC, L, KA, KB, F, P = 10, 2, 5, 20, 4, 10, 256, 128
NB = 2
BW = KB * F // NB

SCRATCH = {
    "asb": ("sbuf", [P, KA * P], "bfloat16"),
    "bsb": ("sbuf", [P, KB * F], "bfloat16"),
    "al": ("sbuf", [P, GR * KB * P], "bfloat16"),
    "ps": ("sbuf", [P, F], "bfloat16"),
    "pl": ("sbuf", [P, F], "bfloat16"),
    "ysb": ("sbuf", [P, F], "bfloat16"),
    "pp": ("psum", [P, 512], "float32"),
    "po": ("psum", [P, 512], "float32"),
}
SEMAPHORES = ["la", "sent", "mm1", "mm2", "cp", "parr", "ad", "st"] + ["lb%d" % c for c in range(NB)] + [
    "ar%d" % s for s in range(N)]


def _bits(m):
    return bin(m).count("1")


def _mask(topo, cores, src, dst):
    m = topo.mask(src, dst)
    if topo.chip(src) == topo.chip(dst):
        for o in cores:
            if topo.chip(o) != topo.chip(src):
                m &= ~topo.mask(src, o)
    return m


def _plan(cores, topo):
    blocks = []
    for s in range(N):
        i, c = divmod(s, GC)
        for R in range(GR):
            ts = [t for t in range(KA) if (KA * c + t) // KB == R]
            if ts:
                blocks.append({"id": len(blocks), "s": s, "R": R, "t0": ts[0], "n": len(ts),
                               "slot": i * KB + KA * c + ts[0] - KB * R, "urgent": i != R})
    sends = [[] for _ in range(N)]
    fwds = [[] for _ in range(N)]
    when = {}
    for s in range(N):
        here, t, near = topo.chip(cores[s]), 0.0, []
        for b in sorted([b for b in blocks if b["s"] == s], key=lambda b: not b["urgent"]):
            row = list(range(b["R"] * GC, (b["R"] + 1) * GC))
            if b["R"]:
                row.reverse()
            chips = []
            for d in row:
                if d != s and topo.chip(cores[d]) not in chips:
                    chips.append(topo.chip(cores[d]))
            groups = [[d for d in row if d != s and topo.chip(cores[d]) == ch] for ch in chips]
            near += [(b, d) for m in groups for d in m if topo.chip(cores[d]) == here]
            far = [m for m in groups if topo.chip(cores[m[0]]) != here]
            many, one = [m for m in far if len(m) > 1], [m for m in far if len(m) == 1]
            if b["urgent"] and b["n"] < KA:
                many.reverse()
                far = many[:1] + one + many[1:]
            else:
                far = many + one
            for m in far:
                same = [d for d in m if topo.die(cores[d]) == topo.die(cores[s])]
                p = same[0] if same else m[0]
                t += b["n"] / KA
                sends[s].append((b, p))
                when[(b["id"], p)] = t
                fwds[p] += [(b, d) for d in m if d != p]
        for b, d in near:
            sends[s].append((b, d))
            when[(b["id"], d)] = 0.3 + 0.5 * b["n"] / KA
    for p in range(N):
        fwds[p].sort(key=lambda e: (not e[0]["urgent"], when[(e[0]["id"], p)]))
        t = 0.0
        for b, d in fwds[p]:
            t = max(t, when[(b["id"], p)] + 0.8) + 0.5 * b["n"] / KA
            when[(b["id"], d)] = t
    order = []
    for r in range(N):
        mine = [b for b in blocks if b["R"] == r // GC]
        key = lambda b: -1.0 if b["s"] == r else when[(b["id"], r)]
        order.append((sorted([b for b in mine if b["urgent"]], key=key), sorted([b for b in mine if not b["urgent"]], key=key)))
    return sends, fwds, order


def rank_program(g, core, T, topo):
    me = T.rank_of(core)
    if me is None:
        return
    cores = list(T.cores)
    sends, fwds, order = _plan(cores, topo)
    sem = T.sem
    urgent, calm = order[me]
    own = [b for b in calm if b["s"] == me]
    seq = own + urgent + [b for b in calm if b["s"] != me]

    def cols(b):
        return slice(b["slot"] * P, (b["slot"] + b["n"]) * P)

    g.sync.dma_start(T.asb[:], T.a[:]).then_inc(sem.la, 16)
    first = (seq[0]["slot"] % KB) * F // BW
    for c in [first] + [c for c in range(NB) if c != first]:
        g.sync.dma_start(T.bsb[:, c * BW:(c + 1) * BW], T.b[:, c * BW:(c + 1) * BW]).then_inc(sem["lb%d" % c], 16)

    sent = [0]

    def put(dst_rank, out_ap, in_ap, rsem):
        dst = cores[dst_rank]
        if not topo.may_write(core, dst):
            raise ValueError("core %d may not write to core %d" % (core, dst))
        m = _mask(topo, cores, core, dst)
        rid, pid, _ = topo.addr(dst)
        g.remote_dma(out_ap=out_ap, in_ap=in_ap, remote_sem=rsem, local_sem=sem.sent, pid=pid, routing_id=rid,
                     dma_engine_mask=m)
        sent[0] += _bits(m)

    def source(b):
        for p in range(N):
            if any(e[0]["id"] == b["id"] and e[1] == me for e in sends[p] + fwds[p]):
                return p
        raise ValueError("block %d never reaches rank %d" % (b["id"], me))

    def count(b):
        return _bits(_mask(topo, cores, cores[source(b)], core))

    g.wait_ge(sem.la, 16)
    for b, d in sends[me]:
        put(d, T.al[:, cols(b)], T.asb[:, b["t0"] * P:(b["t0"] + b["n"]) * P], sem["ar%d" % me])
    for b, d in fwds[me]:
        g.wait_ge(sem["ar%d" % b["s"]], count(b))
        put(d, T.al[:, cols(b)], T.al[:, cols(b)], sem["ar%d" % b["s"]])
    partner = (me + GC) % N
    g.wait_ge(sem.cp, 1)
    put(partner, T.pl[:], T.ps[:], sem.parr)
    g.wait_ge(sem.sent, sent[0])

    left = {True: sum(b["n"] for b in urgent), False: sum(b["n"] for b in calm)}
    total = dict(left)
    have = set()
    for b in seq:
        if b["s"] == me:
            g.tensor.wait_ge(sem.la, 16)
        else:
            g.tensor.wait_ge(sem["ar%d" % b["s"]], count(b))
        for t in range(b["n"]):
            slot = b["slot"] + t
            kk = slot % KB
            if kk * F // BW not in have:
                have.add(kk * F // BW)
                g.tensor.wait_ge(sem["lb%d" % (kk * F // BW)], 16)
            u = b["urgent"]
            lhs = T.asb[:, (b["t0"] + t) * P:(b["t0"] + t + 1) * P] if b["s"] == me else T.al[:, slot * P:(slot + 1) * P]
            mm = g.tensor.matmul((T.pp if u else T.po)[:, 0:F], lhs, T.bsb[:, kk * F:(kk + 1) * F],
                                 left[u] == total[u], left[u] == 1)
            left[u] -= 1
            if left[u] == 0:
                mm.then_inc(sem.mm1 if u else sem.mm2, 1)

    g.vector.wait_ge(sem.mm1, 1)
    g.vector.tensor_copy(T.ps[:], T.pp[:, 0:F]).then_inc(sem.cp, 1)
    g.vector.wait_ge(sem.mm2, 1)
    g.vector.wait_ge(sem.parr, _bits(_mask(topo, cores, cores[partner], core)))
    g.vector.tensor_tensor(T.ysb[:], T.po[:, 0:F], T.pl[:], AluOpType.add).then_inc(sem.ad, 1)

    g.sync.wait_ge(sem.ad, 1)
    g.sync.dma_start(T.y[:], T.ysb[:]).then_inc(sem.st, 16)
    g.sync.wait_ge(sem.st, 16)
